import numpy as np
import ml_dtypes


def mxq(x, axis, fmt="e4m3"):
    dtype, down = {"e4m3": (ml_dtypes.float8_e4m3fn, 7), "e5m2": (ml_dtypes.float8_e5m2, 14)}[fmt]
    v = np.moveaxis(np.asarray(x, np.float32).astype(ml_dtypes.bfloat16).astype(np.float64), axis, -1)
    blocks = v.reshape(v.shape[:-1] + (-1, 32))
    amax = np.abs(blocks).max(-1, keepdims=True)
    byte = np.maximum(np.where(amax > 0, np.frexp(amax)[1] - 1 + 127, 0) - down, 1)
    scale = np.exp2(byte - 127.0)
    codes = (blocks / scale).astype(np.float32).astype(dtype).astype(np.float64)
    return np.moveaxis((codes * scale).reshape(v.shape), -1, axis)


WIDE = False


def mx_kscale(k):
    if not WIDE:
        return np.ones(k)
    levels = np.array([10, -10, 5, -5, 0])
    if k % 512:
        return np.exp2(np.random.permutation(np.resize(levels, k // 32))).repeat(32)
    a = np.empty((k // 512, 16))
    for p in range(k // 512):
        a[p, :8] = np.random.permutation(np.resize(levels, 8))
        for g in range(8):
            far = levels[np.abs(levels - a[p, g]) >= 10]
            a[p, g + 8] = far[np.random.randint(len(far))]
    return np.exp2(a.ravel()).repeat(32)


def f64(x):
    return np.asarray(x).astype(np.float64)


def striped(idx):
    return np.tile(np.asarray(idx).reshape(-1, 16).T, (8, 1)).astype(np.uint16)


def unstriped(offs):
    return offs[:16].T.reshape(-1).astype(np.int64)


E2M1 = np.array([0.0, 0.5, 1.0, 1.5, 2.0, 3.0, 4.0, 6.0, -0.0, -0.5, -1.0, -1.5, -2.0, -3.0, -4.0, -6.0])


def pack_weight(w, fmt):
    k, n = w.shape
    w = f64(np.asarray(w, np.float32).astype(ml_dtypes.bfloat16)).reshape(k // 32, 32, n)
    amax = np.abs(w).max(1)
    if fmt == "e4m3":
        byte = np.frexp(amax)[1] - 1 + 127 - 7
    else:
        mant, ex = np.frexp(amax / 6.0)
        byte = np.where(mant > 0.5, ex, ex - 1) + 127
    byte = np.clip(np.where(amax > 0, byte, 1), 1, 254)
    scaled = (w * np.exp2(127.0 - byte)[:, None, :]).reshape(k, n).astype(np.float32)
    by_word = np.ascontiguousarray(scaled.reshape(k // 512, 128, 4, n).transpose(0, 1, 3, 2))
    if fmt == "e4m3":
        words = by_word.astype(ml_dtypes.float8_e4m3fn).view(np.uint8)
    else:
        c = by_word.astype(ml_dtypes.float4_e2m1fn).view(np.uint8) & 0xF
        words = (c[..., 0::2] | (c[..., 1::2] << 4)).reshape(k // 512, 128, 2 * n)
    return np.ascontiguousarray(words), np.ascontiguousarray(byte.astype(np.uint8).reshape(k // 512, 16, n))


def unpack_weight(words, scales, fmt):
    g, _, n = scales.shape
    words = np.ascontiguousarray(words).reshape(g, 128, n, -1)
    if fmt == "e4m3":
        vals = words.view(ml_dtypes.float8_e4m3fn).astype(np.float64)
    else:
        nib = np.empty((g, 128, n, 4), np.uint8)
        nib[..., 0::2] = words & 0xF
        nib[..., 1::2] = words >> 4
        vals = E2M1[nib]
    vals = vals * np.repeat(np.exp2(scales.astype(np.float64) - 127.0), 8, axis=1)[..., None]
    return vals.transpose(0, 1, 3, 2).reshape(g * 512, n)


def sigmoid(v):
    return 1.0 / (1.0 + np.exp(-v))


D, T, I, Q, E, U, M, C = 512, 2048, 512, 256, 512, 1024, 1024, 512


def setup_inputs():
    n = np.random.standard_normal
    idx = np.random.permutation(T)[:I]
    idx2 = np.random.permutation(U)[:I]
    idx3 = np.random.permutation(M)[:Q]
    fd = mx_kscale(D)
    fi = mx_kscale(I)
    fc = mx_kscale(C)
    ti = np.ones(T)
    ti[idx] = fi
    keysp = pack_weight(n((D, T)) / fd[:, None], "e4m3")
    return {
        "query": (n((D, Q)) * 0.7 / np.sqrt(D) * fd[:, None]).astype(np.float32),
        "query2": (n((D, Q)) * 0.7 / np.sqrt(D) * fd[:, None]).astype(np.float32),
        "keys_words": keysp[0],
        "keys_scales": keysp[1],
        "notes": (n((D, U)) / fd[:, None]).astype(np.float32),
        "os": (np.random.uniform(0.02, 0.08, (1, I)) * fi).astype(np.float32),
        "vals": (n((E, T)) / ti).astype(np.float32),
        "wm": (n((C, E)) * 1.0 / np.sqrt(C) * fc[:, None]).astype(np.float32),
        "mstore": (n((C, M)) / fc[:, None]).astype(np.float32),
        "offs": striped(idx),
        "offs2": striped(idx2),
        "offs3": striped(idx3),
    }


def reference(query, query2, keys_words, keys_scales, notes, os, vals, wm, mstore, offs, offs2, offs3):
    idx = unstriped(offs)
    idx2 = unstriped(offs2)
    idx3 = unstriped(offs3)
    keysu = unpack_weight(keys_words, keys_scales, "e4m3")
    queryq = mxq(f64(query), 0, "e4m3")
    keysidxg = keysu[:, idx]
    query2q = mxq(f64(query2), 0, "e4m3")
    notesidx2q = mxq(f64(notes)[:, idx2], 0, "e4m3")
    s = queryq.T @ keysidxg + query2q.T @ notesidx2q
    w = sigmoid(s)
    wo1 = w * f64(os)
    wt1 = wo1.T
    vt1 = f64(vals)[:, idx].T
    vt1q = mxq(vt1, 0, "e4m3")
    wt1q = mxq(wt1, 0, "e4m3")
    o = vt1q.T @ wt1q
    wmq = mxq(f64(wm), 0, "e4m3")
    mstoreq = mxq(f64(mstore), 0, "e4m3")
    me = wmq.T @ mstoreq
    y = o * me[:, idx3]
    return y

@@ -1,0 +1,225 @@
+from contextlib import ExitStack
+
+import concourse.mybir as mybir
+from concourse.masks import make_identity
+
+D, T, I, Q, E, U, M, C = 512, 2048, 512, 256, 512, 1024, 1024, 512
+FLOPS = 2 * (2 * D * Q * I + I * E * Q + C * E * M)
+
+F32 = mybir.dt.float32
+BF16 = mybir.dt.bfloat16
+I32 = mybir.dt.int32
+U32 = mybir.dt.uint32
+U16 = mybir.dt.uint16
+U8 = mybir.dt.uint8
+FP8X4 = mybir.dt.float8_e4m3fn_x4
+COPY = mybir.ActivationFunctionType.Copy
+SIGMOID = mybir.ActivationFunctionType.Sigmoid
+MULT = mybir.AluOpType.mult
+
+P = 128
+PACK = 4
+BANK = 512
+LIST_ROWS = 16
+POOL_BYTES = 4 * T
+
+
+def tile_attend_twosources_remembered_lean_kernel(
+    tc, query, query2, keys_words, keys_scales, notes, slot_factor, vals, wm, mstore, offs, offs2, offs3, out
+):
+    nc = tc.nc
+    with ExitStack() as ctx:
+        lists = ctx.enter_context(tc.tile_pool(name="lists", bufs=1))
+        sb = ctx.enter_context(tc.tile_pool(name="sb", bufs=1))
+        values = ctx.enter_context(tc.tile_pool(name="values", bufs=1))
+        psum = ctx.enter_context(tc.psum_pool(name="psum", bufs=2))
+
+        def load_rows(src, name):
+            width = src.shape[1]
+            raw = sb.tile([P, PACK, width], F32, name=name)
+            nc.sync.dma_start(out=raw[:], in_=src.rearrange("(p j) w -> p j w", j=PACK))
+            return raw
+
+        def load_list(src, name):
+            offsets = lists.tile([P, src.shape[1]], U16, name=name)
+            nc.sync.dma_start(offsets[:], src)
+            return offsets
+
+        def interleave(raw, name):
+            width = raw.shape[2]
+            grouped = sb.tile([P, width, PACK], BF16, name=name, align_bytes=64)
+            nc.vector.tensor_copy(
+                out=grouped[:].rearrange("p (c i) j -> p c j i", i=PACK),
+                in_=raw[:].rearrange("p j (c i) -> p c j i", i=PACK),
+            )
+            return grouped
+
+        def quantise(grouped, name, codes=None):
+            width = grouped.shape[1]
+            if codes is None:
+                codes = sb.tile([P, width], U32, name=name + "_codes", align_bytes=64)
+            scales = sb.tile([P, width], U8, name=name + "_scales", align_bytes=64)
+            nc.vector.quantize_mx(
+                out=codes[:].bitcast(FP8X4), scales=scales[:], in_=grouped[:].rearrange("p w j -> p (w j)")
+            )
+            return codes, scales
+
+        def product(acc, stationary, cols, moving, start, stop):
+            nc.tensor.matmul_mx(
+                out=acc,
+                lhsT=stationary[0][:, cols].bitcast(FP8X4),
+                lhsT_scale=stationary[1][:, cols],
+                rhs=moving[0][:].bitcast(FP8X4),
+                rhs_scale=moving[1][:],
+                start=start,
+                stop=stop,
+            )
+
+        key_scale_pool = sb.tile([P, T], U8, name="key_scale_pool")
+        nc.vector.memset(key_scale_pool[:].bitcast(I32), 0)
+        identity = sb.tile([P, P], F32, name="identity")
+        make_identity(nc, identity[:])
+
+        note_rows = notes.rearrange("(p j) u -> j p u", j=PACK)
+
+        def load_notes(j):
+            plane = sb.tile([P, U], F32, name="note_pool%d" % j)
+            nc.sync.dma_start(out=plane[:], in_=note_rows[j])
+            return plane
+
+        def load_store(h):
+            return load_rows(mstore[:, h * BANK : (h + 1) * BANK], "store_raw%d" % h)
+
+        note_list = load_list(offs2, "note_list")
+        note_pool = [load_notes(0)]
+        wm_raw = load_rows(wm, "wm_raw")
+        for r in range(4):
+            nc.sync.dma_start(
+                out=key_scale_pool[r:P:32, :].bitcast(I32), in_=keys_scales[0, r:16:4, :].bitcast(I32)
+            )
+        token_list = load_list(offs, "token_list")
+        note_pool.append(load_notes(1))
+        store_raw = [load_store(0)]
+        note_pool.append(load_notes(2))
+        store_raw.append(load_store(1))
+        memory_list = load_list(offs3, "memory_list")
+        note_pool.append(load_notes(3))
+        query2_raw = load_rows(query2, "query2_raw")
+        factor = sb.tile([P, 1, PACK], F32, name="factor")
+        nc.sync.dma_start(out=factor[:, 0, :], in_=slot_factor.rearrange("o (p j) -> (o p) j", j=PACK))
+        key_word_pool = sb.tile([P, T], U32, name="key_word_pool")
+        nc.sync.dma_start(
+            out=key_word_pool[:].bitcast(I32), in_=keys_words[0].rearrange("p t j -> p (t j)").bitcast(I32)
+        )
+        query_raw = load_rows(query, "query_raw")
+        value_pool = []
+        for t in range(E // P):
+            rows = values.tile([P, T], F32, name="value_pool%d" % t, align_bytes=64, offset=t * POOL_BYTES)
+            nc.sync.dma_start(out=rows[:], in_=vals[t * P : (t + 1) * P, :])
+            value_pool.append(rows)
+
+        note_picked = sb.tile([P, PACK, I], BF16, name="note_picked")
+
+        def pick_notes(j):
+            nc.scalar.activation(note_picked[:, j, :], note_pool[j][:].indirect(note_list[:]), COPY)
+
+        memory = [sb.tile([P, M], F32, name="memory%d" % t) for t in range(E // P)]
+
+        def make_memories(h):
+            store_q = quantise(interleave(store_raw[h], "store_bf%d" % h), "store%d" % h)
+            for t in range(E // P):
+                bank = psum.tile([P, BANK], F32, name="memory_bank%d" % t, tag="bank%d" % t, bufs=1)
+                product(bank[:], wm_q, slice(t * P, (t + 1) * P), store_q, True, True)
+                nc.scalar.copy(out=memory[t][:, h * BANK : (h + 1) * BANK], in_=bank[:])
+
+        pick_notes(0)
+        wm_q = quantise(interleave(wm_raw, "wm_bf"), "wm")
+        pick_notes(1)
+        key_scales = sb.tile([P, I], U8, name="key_scales", align_bytes=64)
+        nc.vector.tensor_copy(key_scales[:], key_scale_pool[:].indirect(token_list[:]))
+        pick_notes(2)
+        make_memories(0)
+        pick_notes(3)
+        make_memories(1)
+
+        query2_bf = interleave(query2_raw, "query2_bf")
+        note_bf = interleave(note_picked, "note_bf")
+        query2_q = quantise(query2_bf, "query2")
+        note_q = quantise(note_bf, "note")
+        scores = [psum.tile([P, I], F32, name="score_bank%d" % h, tag="score") for h in range(Q // P)]
+        for h in range(Q // P):
+            product(scores[h][:], query2_q, slice(h * P, (h + 1) * P), note_q, True, False)
+        query_bf = interleave(query_raw, "query_bf")
+        key_words = sb.tile([P, I], U32, name="key_words", align_bytes=64)
+        nc.vector.tensor_copy(key_words[:], key_word_pool[:].indirect(token_list[:]))
+        query_q = quantise(query_bf, "query")
+        for h in range(Q // P):
+            product(scores[h][:], query_q, slice(h * P, (h + 1) * P), (key_words, key_scales), False, True)
+
+        picked_memory = []
+        for t in range(E // P):
+            picked = sb.tile([P, Q], F32, name="picked_memory%d" % t)
+            nc.scalar.activation(picked[:], memory[t][:].indirect(memory_list[:]), COPY)
+            picked_memory.append(picked)
+
+        half = I // 2
+        tiles = E // P
+
+        def pick_values(t, vector_share):
+            picked = sb.tile([P, I], BF16, name="value_picked%d" % t)
+            cut = vector_share // LIST_ROWS
+            if vector_share > 0:
+                nc.vector.tensor_copy(picked[:, :vector_share], value_pool[t][:].indirect(token_list[:, :cut]))
+            if vector_share < I:
+                nc.scalar.activation(picked[:, vector_share:], value_pool[t][:].indirect(token_list[:, cut:]), COPY)
+            pairs = picked[:].bitcast(F32)
+            turned = psum.tile([P, 2, P], F32, name="value_bank%d" % t, tag="bank%d" % t, bufs=1)
+            for u in range(2):
+                nc.tensor.transpose(turned[:, u, :], pairs[:, u : I // 2 : 2], identity[:])
+            value_bf = sb.tile([P, P, PACK], BF16, name="value_bf%d" % t, align_bytes=64)
+            nc.scalar.copy(
+                out=value_bf[:].rearrange("p e j -> p (e j)").bitcast(F32).rearrange("p (e u) -> p e u", u=2),
+                in_=turned[:].rearrange("p u e -> p e u"),
+            )
+            return value_bf
+
+        values_bf = [pick_values(0, 0), pick_values(1, I)]
+        weight_bf = values.tile([P, Q, PACK], BF16, name="weight_bf", align_bytes=64, offset=POOL_BYTES + 1024)
+        for h in range(Q // P):
+            gate = values.tile([P, PACK, P], F32, name="gate%d" % h, align_bytes=64, offset=h * 4 * I)
+            nc.scalar.activation(
+                gate[:].rearrange("p j s -> p s j"), scores[h][:].rearrange("p (s j) -> p s j", j=PACK), SIGMOID
+            )
+            turned = psum.tile([P, PACK, P], F32, name="gate_bank")
+            for j in range(PACK):
+                nc.tensor.transpose(turned[:, j, :], gate[:, j, :], identity[:])
+            nc.vector.tensor_tensor(
+                weight_bf[:, h * P : (h + 1) * P, :],
+                turned[:].rearrange("p j q -> p q j"),
+                factor[:].to_broadcast([P, P, PACK]),
+                MULT,
+            )
+        weight_q = quantise(weight_bf, "weight")
+
+        def read_values(t, over):
+            codes = values.tile([P, P], U32, name="value_codes%d" % t, align_bytes=64, offset=over * POOL_BYTES + t * 4 * P)
+            value_q = quantise(values_bf[t], "value%d" % t, codes)
+            read = psum.tile([P, Q], F32, name="read_bank%d" % t, tag="bank%d" % t, bufs=1)
+            product(read[:], value_q, slice(0, P), weight_q, True, True)
+            return read
+
+        def finish(t):
+            result = values.tile(
+                [P, Q], F32, name="result%d" % t, align_bytes=64, offset=3 * POOL_BYTES + (t + 2) * 4 * Q
+            )
+            nc.vector.tensor_tensor(result[:], reads[t][:], picked_memory[t][:], MULT)
+            nc.sync.dma_start(out=out[t * P : (t + 1) * P, :], in_=result[:])
+
+        values_bf.append(pick_values(2, 0))
+        reads = [read_values(0, 2), read_values(1, 2)]
+        values_bf.append(pick_values(3, half))
+        reads.append(read_values(2, 3))
+        for t in range(3):
+            finish(t)
+        reads.append(read_values(3, 4))
+        finish(3)

@@ -77,6 +77,10 @@ def tile_attend_twosources_remembered_lean_kernel(
 
         key_scale_pool = sb.tile([P, T], U8, name="key_scale_pool")
         nc.vector.memset(key_scale_pool[:].bitcast(I32), 0)
+        warm_in = sb.tile([P, 1], F32, name="warm_in")
+        nc.gpsimd.memset(warm_in[:], 0.0)
+        warm_out = sb.tile([P, 1], F32, name="warm_out")
+        nc.scalar.activation(warm_out[:], warm_in[:], SIGMOID)
         identity = sb.tile([P, P], F32, name="identity")
         make_identity(nc, identity[:])
 

@@ -94,8 +94,8 @@ def tile_attend_twosources_remembered_lean_kernel(
         def load_store(h):
             return load_rows(mstore[:, h * BANK : (h + 1) * BANK], "store_raw%d" % h)
 
-        note_list = load_list(offs2, "note_list")
         note_pool = [load_notes(0)]
+        note_list = load_list(offs2, "note_list")
         wm_raw = load_rows(wm, "wm_raw")
         for r in range(4):
             nc.sync.dma_start(
@@ -180,17 +180,24 @@ def tile_attend_twosources_remembered_lean_kernel(
             turned = psum.tile([P, 2, P], F32, name="value_bank%d" % t, tag="bank%d" % t, bufs=1)
             for u in range(2):
                 nc.tensor.transpose(turned[:, u, :], pairs[:, u : I // 2 : 2], identity[:])
-            value_bf = sb.tile([P, P, PACK], BF16, name="value_bf%d" % t, align_bytes=64)
+            return turned
+
+        def round_values(t):
+            turned = values_turned[t]
+            value_bf = values.tile(
+                [P, P, PACK], BF16, name="value_bf%d" % t, align_bytes=64, offset=(t + 1) * POOL_BYTES + 7 * 1024
+            )
             nc.scalar.copy(
                 out=value_bf[:].rearrange("p e j -> p (e j)").bitcast(F32).rearrange("p (e u) -> p e u", u=2),
                 in_=turned[:].rearrange("p u e -> p e u"),
             )
             return value_bf
 
-        values_bf = [pick_values(0, 0), pick_values(1, I)]
+        values_turned = [pick_values(0, I), pick_values(1, I)]
+        values_bf = [round_values(0)]
         weight_bf = values.tile([P, Q, PACK], BF16, name="weight_bf", align_bytes=64, offset=POOL_BYTES + 1024)
         for h in range(Q // P):
-            gate = values.tile([P, PACK, P], F32, name="gate%d" % h, align_bytes=64, offset=h * 4 * I)
+            gate = sb.tile([P, PACK, P], F32, name="gate%d" % h)
             nc.scalar.activation(
                 gate[:].rearrange("p j s -> p s j"), scores[h][:].rearrange("p (s j) -> p s j", j=PACK), SIGMOID
             )
@@ -219,9 +226,12 @@ def tile_attend_twosources_remembered_lean_kernel(
             nc.vector.tensor_tensor(result[:], reads[t][:], picked_memory[t][:], MULT)
             nc.sync.dma_start(out=out[t * P : (t + 1) * P, :], in_=result[:])
 
-        values_bf.append(pick_values(2, 0))
+        values_turned.append(pick_values(2, 0))
+        values_bf.append(round_values(1))
         reads = [read_values(0, 2), read_values(1, 2)]
-        values_bf.append(pick_values(3, half))
+        values_turned.append(pick_values(3, half))
+        values_bf.append(round_values(2))
+        values_bf.append(round_values(3))
         reads.append(read_values(2, 3))
         for t in range(3):
             finish(t)

@@ -50,7 +50,7 @@ def tile_attend_twosources_remembered_lean_kernel(
             grouped = sb.tile([P, width, PACK], BF16, name=name, align_bytes=64)
             nc.vector.tensor_copy(
                 out=grouped[:].rearrange("p (c i) j -> p c j i", i=PACK),
-                in_=raw[:].rearrange("p j (c i) -> p c j i", i=PACK),
+                in_=raw.rearrange("p j (c i) -> p c j i", i=PACK),
             )
             return grouped
 
@@ -91,23 +91,16 @@ def tile_attend_twosources_remembered_lean_kernel(
             nc.sync.dma_start(out=plane[:], in_=note_rows[j])
             return plane
 
-        def load_store(h):
-            return load_rows(mstore[:, h * BANK : (h + 1) * BANK], "store_raw%d" % h)
-
-        note_pool = [load_notes(0)]
-        note_list = load_list(offs2, "note_list")
         wm_raw = load_rows(wm, "wm_raw")
         for r in range(4):
             nc.sync.dma_start(
                 out=key_scale_pool[r:P:32, :].bitcast(I32), in_=keys_scales[0, r:16:4, :].bitcast(I32)
             )
         token_list = load_list(offs, "token_list")
-        note_pool.append(load_notes(1))
-        store_raw = [load_store(0)]
-        note_pool.append(load_notes(2))
-        store_raw.append(load_store(1))
+        store_raw = load_rows(mstore, "store_raw")
+        note_list = load_list(offs2, "note_list")
+        note_pool = [load_notes(j) for j in range(PACK)]
         memory_list = load_list(offs3, "memory_list")
-        note_pool.append(load_notes(3))
         query2_raw = load_rows(query2, "query2_raw")
         factor = sb.tile([P, 1, PACK], F32, name="factor")
         nc.sync.dma_start(out=factor[:, 0, :], in_=slot_factor.rearrange("o (p j) -> (o p) j", j=PACK))
@@ -130,30 +123,29 @@ def tile_attend_twosources_remembered_lean_kernel(
         memory = [sb.tile([P, M], F32, name="memory%d" % t) for t in range(E // P)]
 
         def make_memories(h):
-            store_q = quantise(interleave(store_raw[h], "store_bf%d" % h), "store%d" % h)
+            store_q = quantise(interleave(store_raw[:, :, h * BANK : (h + 1) * BANK], "store_bf%d" % h), "store%d" % h)
             for t in range(E // P):
                 bank = psum.tile([P, BANK], F32, name="memory_bank%d" % t, tag="bank%d" % t, bufs=1)
                 product(bank[:], wm_q, slice(t * P, (t + 1) * P), store_q, True, True)
                 nc.scalar.copy(out=memory[t][:, h * BANK : (h + 1) * BANK], in_=bank[:])
 
-        pick_notes(0)
-        wm_q = quantise(interleave(wm_raw, "wm_bf"), "wm")
-        pick_notes(1)
+        wm_q = quantise(interleave(wm_raw[:], "wm_bf"), "wm")
         key_scales = sb.tile([P, I], U8, name="key_scales", align_bytes=64)
         nc.vector.tensor_copy(key_scales[:], key_scale_pool[:].indirect(token_list[:]))
-        pick_notes(2)
-        make_memories(0)
-        pick_notes(3)
-        make_memories(1)
+        for j in range(PACK - 1):
+            pick_notes(j)
+        for h in range(M // BANK):
+            make_memories(h)
+        nc.vector.tensor_copy(note_picked[:, PACK - 1, :], note_pool[PACK - 1][:].indirect(note_list[:]))
 
-        query2_bf = interleave(query2_raw, "query2_bf")
-        note_bf = interleave(note_picked, "note_bf")
+        query2_bf = interleave(query2_raw[:], "query2_bf")
+        note_bf = interleave(note_picked[:], "note_bf")
         query2_q = quantise(query2_bf, "query2")
         note_q = quantise(note_bf, "note")
         scores = [psum.tile([P, I], F32, name="score_bank%d" % h, tag="score") for h in range(Q // P)]
         for h in range(Q // P):
             product(scores[h][:], query2_q, slice(h * P, (h + 1) * P), note_q, True, False)
-        query_bf = interleave(query_raw, "query_bf")
+        query_bf = interleave(query_raw[:], "query_bf")
         key_words = sb.tile([P, I], U32, name="key_words", align_bytes=64)
         nc.vector.tensor_copy(key_words[:], key_word_pool[:].indirect(token_list[:]))
         query_q = quantise(query_bf, "query")

from contextlib import ExitStack

import concourse.mybir as mybir
from concourse.masks import make_identity

D, T, I, Q, E, U, M, C = 512, 2048, 512, 256, 512, 1024, 1024, 512
FLOPS = 2 * (2 * D * Q * I + I * E * Q + C * E * M)

F32 = mybir.dt.float32
BF16 = mybir.dt.bfloat16
I32 = mybir.dt.int32
U32 = mybir.dt.uint32
U16 = mybir.dt.uint16
U8 = mybir.dt.uint8
FP8X4 = mybir.dt.float8_e4m3fn_x4
COPY = mybir.ActivationFunctionType.Copy
SIGMOID = mybir.ActivationFunctionType.Sigmoid
MULT = mybir.AluOpType.mult

P = 128
PACK = 4
BANK = 512
LIST_ROWS = 16
POOL_BYTES = 4 * T


def tile_attend_twosources_remembered_lean_kernel(
    tc, query, query2, keys_words, keys_scales, notes, slot_factor, vals, wm, mstore, offs, offs2, offs3, out
):
    nc = tc.nc
    with ExitStack() as ctx:
        lists = ctx.enter_context(tc.tile_pool(name="lists", bufs=1))
        sb = ctx.enter_context(tc.tile_pool(name="sb", bufs=1))
        values = ctx.enter_context(tc.tile_pool(name="values", bufs=1))
        psum = ctx.enter_context(tc.psum_pool(name="psum", bufs=2))

        def load_rows(src, name):
            width = src.shape[1]
            raw = sb.tile([P, PACK, width], F32, name=name)
            nc.sync.dma_start(out=raw[:], in_=src.rearrange("(p j) w -> p j w", j=PACK))
            return raw

        def load_list(src, name):
            offsets = lists.tile([P, src.shape[1]], U16, name=name)
            nc.sync.dma_start(offsets[:], src)
            return offsets

        def interleave(raw, name):
            width = raw.shape[2]
            grouped = sb.tile([P, width, PACK], BF16, name=name, align_bytes=64)
            nc.vector.tensor_copy(
                out=grouped[:].rearrange("p (c i) j -> p c j i", i=PACK),
                in_=raw.rearrange("p j (c i) -> p c j i", i=PACK),
            )
            return grouped

        def quantise(grouped, name, codes=None):
            width = grouped.shape[1]
            if codes is None:
                codes = sb.tile([P, width], U32, name=name + "_codes", align_bytes=64)
            scales = sb.tile([P, width], U8, name=name + "_scales", align_bytes=64)
            nc.vector.quantize_mx(
                out=codes[:].bitcast(FP8X4), scales=scales[:], in_=grouped[:].rearrange("p w j -> p (w j)")
            )
            return codes, scales

        def product(acc, stationary, cols, moving, start, stop):
            nc.tensor.matmul_mx(
                out=acc,
                lhsT=stationary[0][:, cols].bitcast(FP8X4),
                lhsT_scale=stationary[1][:, cols],
                rhs=moving[0][:].bitcast(FP8X4),
                rhs_scale=moving[1][:],
                start=start,
                stop=stop,
            )

        key_scale_pool = sb.tile([P, T], U8, name="key_scale_pool")
        nc.vector.memset(key_scale_pool[:].bitcast(I32), 0)
        warm_in = sb.tile([P, 1], F32, name="warm_in")
        nc.gpsimd.memset(warm_in[:], 0.0)
        warm_out = sb.tile([P, 1], F32, name="warm_out")
        nc.scalar.activation(warm_out[:], warm_in[:], SIGMOID)
        identity = sb.tile([P, P], F32, name="identity")
        make_identity(nc, identity[:])

        note_rows = notes.rearrange("(p j) u -> j p u", j=PACK)

        def load_notes(j):
            plane = sb.tile([P, U], F32, name="note_pool%d" % j)
            nc.sync.dma_start(out=plane[:], in_=note_rows[j])
            return plane

        wm_raw = load_rows(wm, "wm_raw")
        for r in range(4):
            nc.sync.dma_start(
                out=key_scale_pool[r:P:32, :].bitcast(I32), in_=keys_scales[0, r:16:4, :].bitcast(I32)
            )
        token_list = load_list(offs, "token_list")
        store_raw = load_rows(mstore, "store_raw")
        note_list = load_list(offs2, "note_list")
        note_pool = [load_notes(j) for j in range(PACK)]
        memory_list = load_list(offs3, "memory_list")
        query2_raw = load_rows(query2, "query2_raw")
        factor = sb.tile([P, 1, PACK], F32, name="factor")
        nc.sync.dma_start(out=factor[:, 0, :], in_=slot_factor.rearrange("o (p j) -> (o p) j", j=PACK))
        key_word_pool = sb.tile([P, T], U32, name="key_word_pool")
        nc.sync.dma_start(
            out=key_word_pool[:].bitcast(I32), in_=keys_words[0].rearrange("p t j -> p (t j)").bitcast(I32)
        )
        query_raw = load_rows(query, "query_raw")
        value_pool = []
        for t in range(E // P):
            rows = values.tile([P, T], F32, name="value_pool%d" % t, align_bytes=64, offset=t * POOL_BYTES)
            nc.sync.dma_start(out=rows[:], in_=vals[t * P : (t + 1) * P, :])
            value_pool.append(rows)

        note_picked = sb.tile([P, PACK, I], BF16, name="note_picked")

        def pick_notes(j):
            nc.scalar.activation(note_picked[:, j, :], note_pool[j][:].indirect(note_list[:]), COPY)

        memory = [sb.tile([P, M], F32, name="memory%d" % t) for t in range(E // P)]

        def make_memories(h):
            store_q = quantise(interleave(store_raw[:, :, h * BANK : (h + 1) * BANK], "store_bf%d" % h), "store%d" % h)
            for t in range(E // P):
                bank = psum.tile([P, BANK], F32, name="memory_bank%d" % t, tag="bank%d" % t, bufs=1)
                product(bank[:], wm_q, slice(t * P, (t + 1) * P), store_q, True, True)
                nc.scalar.copy(out=memory[t][:, h * BANK : (h + 1) * BANK], in_=bank[:])

        wm_q = quantise(interleave(wm_raw[:], "wm_bf"), "wm")
        key_scales = sb.tile([P, I], U8, name="key_scales", align_bytes=64)
        nc.vector.tensor_copy(key_scales[:], key_scale_pool[:].indirect(token_list[:]))
        for j in range(PACK - 1):
            pick_notes(j)
        for h in range(M // BANK):
            make_memories(h)
        nc.vector.tensor_copy(note_picked[:, PACK - 1, :], note_pool[PACK - 1][:].indirect(note_list[:]))

        query2_bf = interleave(query2_raw[:], "query2_bf")
        note_bf = interleave(note_picked[:], "note_bf")
        query2_q = quantise(query2_bf, "query2")
        note_q = quantise(note_bf, "note")
        scores = [psum.tile([P, I], F32, name="score_bank%d" % h, tag="score") for h in range(Q // P)]
        for h in range(Q // P):
            product(scores[h][:], query2_q, slice(h * P, (h + 1) * P), note_q, True, False)
        query_bf = interleave(query_raw[:], "query_bf")
        key_words = sb.tile([P, I], U32, name="key_words", align_bytes=64)
        nc.vector.tensor_copy(key_words[:], key_word_pool[:].indirect(token_list[:]))
        query_q = quantise(query_bf, "query")
        for h in range(Q // P):
            product(scores[h][:], query_q, slice(h * P, (h + 1) * P), (key_words, key_scales), False, True)

        picked_memory = []
        for t in range(E // P):
            picked = sb.tile([P, Q], F32, name="picked_memory%d" % t)
            nc.scalar.activation(picked[:], memory[t][:].indirect(memory_list[:]), COPY)
            picked_memory.append(picked)

        half = I // 2
        tiles = E // P

        def pick_values(t, vector_share):
            picked = sb.tile([P, I], BF16, name="value_picked%d" % t)
            cut = vector_share // LIST_ROWS
            if vector_share > 0:
                nc.vector.tensor_copy(picked[:, :vector_share], value_pool[t][:].indirect(token_list[:, :cut]))
            if vector_share < I:
                nc.scalar.activation(picked[:, vector_share:], value_pool[t][:].indirect(token_list[:, cut:]), COPY)
            pairs = picked[:].bitcast(F32)
            turned = psum.tile([P, 2, P], F32, name="value_bank%d" % t, tag="bank%d" % t, bufs=1)
            for u in range(2):
                nc.tensor.transpose(turned[:, u, :], pairs[:, u : I // 2 : 2], identity[:])
            return turned

        def round_values(t):
            turned = values_turned[t]
            value_bf = values.tile(
                [P, P, PACK], BF16, name="value_bf%d" % t, align_bytes=64, offset=(t + 1) * POOL_BYTES + 7 * 1024
            )
            nc.scalar.copy(
                out=value_bf[:].rearrange("p e j -> p (e j)").bitcast(F32).rearrange("p (e u) -> p e u", u=2),
                in_=turned[:].rearrange("p u e -> p e u"),
            )
            return value_bf

        values_turned = [pick_values(0, I), pick_values(1, I)]
        values_bf = [round_values(0)]
        weight_bf = values.tile([P, Q, PACK], BF16, name="weight_bf", align_bytes=64, offset=POOL_BYTES + 1024)
        for h in range(Q // P):
            gate = sb.tile([P, PACK, P], F32, name="gate%d" % h)
            nc.scalar.activation(
                gate[:].rearrange("p j s -> p s j"), scores[h][:].rearrange("p (s j) -> p s j", j=PACK), SIGMOID
            )
            turned = psum.tile([P, PACK, P], F32, name="gate_bank")
            for j in range(PACK):
                nc.tensor.transpose(turned[:, j, :], gate[:, j, :], identity[:])
            nc.vector.tensor_tensor(
                weight_bf[:, h * P : (h + 1) * P, :],
                turned[:].rearrange("p j q -> p q j"),
                factor[:].to_broadcast([P, P, PACK]),
                MULT,
            )
        weight_q = quantise(weight_bf, "weight")

        def read_values(t, over):
            codes = values.tile([P, P], U32, name="value_codes%d" % t, align_bytes=64, offset=over * POOL_BYTES + t * 4 * P)
            value_q = quantise(values_bf[t], "value%d" % t, codes)
            read = psum.tile([P, Q], F32, name="read_bank%d" % t, tag="bank%d" % t, bufs=1)
            product(read[:], value_q, slice(0, P), weight_q, True, True)
            return read

        def finish(t):
            result = values.tile(
                [P, Q], F32, name="result%d" % t, align_bytes=64, offset=3 * POOL_BYTES + (t + 2) * 4 * Q
            )
            nc.vector.tensor_tensor(result[:], reads[t][:], picked_memory[t][:], MULT)
            nc.sync.dma_start(out=out[t * P : (t + 1) * P, :], in_=result[:])

        values_turned.append(pick_values(2, 0))
        values_bf.append(round_values(1))
        reads = [read_values(0, 2), read_values(1, 2)]
        values_turned.append(pick_values(3, half))
        values_bf.append(round_values(2))
        values_bf.append(round_values(3))
        reads.append(read_values(2, 3))
        for t in range(3):
            finish(t)
        reads.append(read_values(3, 4))
        finish(3)
